import numpy as np
import ml_dtypes


def mxq(x, axis, fmt="e4m3"):
    dtype, down = {"e4m3": (ml_dtypes.float8_e4m3fn, 7), "e5m2": (ml_dtypes.float8_e5m2, 14)}[fmt]
    v = np.moveaxis(np.asarray(x, np.float32).astype(ml_dtypes.bfloat16).astype(np.float64), axis, -1)
    blocks = v.reshape(v.shape[:-1] + (-1, 32))
    amax = np.abs(blocks).max(-1, keepdims=True)
    byte = np.maximum(np.where(amax > 0, np.frexp(amax)[1] - 1 + 127, 0) - down, 1)
    scale = np.exp2(byte - 127.0)
    codes = (blocks / scale).astype(np.float32).astype(dtype).astype(np.float64)
    return np.moveaxis((codes * scale).reshape(v.shape), -1, axis)


WIDE = False


def mx_kscale(k):
    if not WIDE:
        return np.ones(k)
    levels = np.array([10, -10, 5, -5, 0])
    if k % 512:
        return np.exp2(np.random.permutation(np.resize(levels, k // 32))).repeat(32)
    a = np.empty((k // 512, 16))
    for p in range(k // 512):
        a[p, :8] = np.random.permutation(np.resize(levels, 8))
        for g in range(8):
            far = levels[np.abs(levels - a[p, g]) >= 10]
            a[p, g + 8] = far[np.random.randint(len(far))]
    return np.exp2(a.ravel()).repeat(32)


def f64(x):
    return np.asarray(x).astype(np.float64)


def striped(idx):
    return np.tile(idx.reshape(-1, 16).T, (8, 1)).astype(np.uint16)


def unstriped(offs):
    return offs[:16].T.reshape(-1).astype(np.int64)


def striped8(idx):
    return np.concatenate([x.reshape(-1, 16).T for x in idx]).astype(np.uint16)


def runs(offs, k):
    lists = np.stack([offs[16 * r : 16 * r + 16].T.reshape(-1) for r in range(8)]).astype(np.int64)
    return lists[np.arange(k) % 512 // 64]


def pack_weight(w):
    k, n = w.shape
    w = f64(np.asarray(w, np.float32).astype(ml_dtypes.bfloat16)).reshape(k // 32, 32, n)
    amax = np.abs(w).max(1)
    byte = np.clip(np.where(amax > 0, np.frexp(amax)[1] - 1 + 127 - 7, 1), 1, 254)
    scaled = (w * np.exp2(127.0 - byte)[:, None, :]).reshape(k, n).astype(np.float32)
    words = np.ascontiguousarray(scaled.reshape(k // 512, 128, 4, n).transpose(0, 1, 3, 2)).astype(ml_dtypes.float8_e4m3fn).view(np.uint8)
    return words, np.ascontiguousarray(byte.astype(np.uint8).reshape(k // 512, 16, n))


def unpack_weight(words, scales):
    g, p, n, _ = words.shape
    vals = np.ascontiguousarray(words).view(ml_dtypes.float8_e4m3fn).astype(np.float64) * np.repeat(np.exp2(scales.astype(np.float64) - 127.0), 8, axis=1)[..., None]
    return vals.transpose(0, 1, 3, 2).reshape(g * 512, n)


def sigmoid(v):
    return 1.0 / (1.0 + np.exp(-np.maximum(v, -700.0)))

def planes(y):
    n, m = y.shape
    v = y.astype(np.float32).astype(ml_dtypes.bfloat16).astype(np.float64).reshape(n // 32, 32, m)
    top = np.abs(v).max(1)
    byte = np.clip(np.where(top > 0, np.frexp(top)[1] - 1 + 127 - 7, 1), 1, 254)
    codes = (v * np.exp2(127.0 - byte)[:, None, :]).reshape(n, m).astype(np.float32).astype(ml_dtypes.float8_e4m3fn).view(np.uint8)
    words = codes.reshape(n // 512, 128, 4, m).transpose(0, 1, 3, 2)
    return np.ascontiguousarray(words), np.ascontiguousarray(byte.astype(np.uint8).reshape(n // 512, 16, m))


K, T, S, H, W = 512, 2048, 512, 512, 256


def setup_inputs():
    n = np.random.standard_normal
    s = mx_kscale(K)[:, None]
    u = mx_kscale(S)
    packed_xT = pack_weight(n((K, T)) * s)
    packed_w1 = pack_weight(n((K, H)) / np.sqrt(K) / s)
    perm = np.stack([np.random.permutation(S) for _ in range(8)])
    return {
        "x_words": packed_xT[0],
        "x_scales": packed_xT[1],
        "w1_words": packed_w1[0],
        "w1_scales": packed_w1[1],
        "ga": (np.random.uniform(0.5, 1.5, (H, 1)) * u[:, None]).astype(np.float32),
        "gb": (np.random.uniform(0.5, 1.5, (H, 1)) / u[:, None]).astype(np.float32),
        "offs": striped(np.random.permutation(T)[:S]),
        "n1": striped8(np.stack([np.random.permutation(S) for _ in range(8)])),
        "n2": striped8(np.stack([np.random.permutation(S) for _ in range(8)])),
        "n3": striped8(np.stack([np.random.permutation(S) for _ in range(8)])),
        "n4": striped8(np.stack([np.random.permutation(S) for _ in range(8)])),
        "n5": striped8(perm[:, :W]),
        "n6": striped8(perm[:, W:]),
        "n7": striped8(np.stack([np.random.permutation(S) for _ in range(8)])),
        "n8": striped8(np.stack([np.random.permutation(S) for _ in range(8)])),
    }


def reference(x_words, x_scales, w1_words, w1_scales, ga, gb, offs, n1, n2, n3, n4, n5, n6, n7, n8):
    xq = unpack_weight(x_words, x_scales)[:, unstriped(offs)]
    y = unpack_weight(w1_words, w1_scales).T @ xq
    z = f64(ga) * (0.75 * ((y[np.arange(H)[:, None], runs(n1, H)]) * (y[np.arange(H)[:, None], runs(n2, H)]) - ((y[np.arange(H)[:, None], runs(n3, H)]) * (y[np.arange(H)[:, None], runs(n4, H)]))))
    pa = y[np.arange(H)[:, None], runs(n5, H)]
    pb = y[np.arange(H)[:, None], runs(n6, H)]
    ra = pa * sigmoid(pb)
    ds = y.copy()
    ds[np.arange(H)[:, None], runs(n6, H)] = ra
    z2 = f64(gb) * ds
    s = 0.0625 * ((mxq(z, 0, "e4m3").T @ mxq(z2, 0, "e4m3")))
    out_0 = np.maximum(s * (sigmoid(s[np.arange(S)[:, None], runs(n7, S)])), s[np.arange(S)[:, None], runs(n8, S)])
    return (out_0,) + planes(out_0)

@@ -1,0 +1,260 @@
+from contextlib import ExitStack
+
+import concourse.mybir as mybir
+
+K, T, S, H, W = 512, 2048, 512, 512, 256
+FLOPS = 2 * K * H * S + 2 * H * S * S
+
+F32 = mybir.dt.float32
+BF16 = mybir.dt.bfloat16
+I32 = mybir.dt.int32
+U32 = mybir.dt.uint32
+U16 = mybir.dt.uint16
+U8 = mybir.dt.uint8
+FP8X4 = mybir.dt.float8_e4m3fn_x4
+ALU = mybir.AluOpType
+ACT = mybir.ActivationFunctionType
+
+P = 128
+PACK = 4
+HALF = S // 2
+WIDE = 2 * S
+PARTS = ((0, 256), (256, 128), (384, 128))
+
+
+def tile_picked_selfdetfoldgmax_none_po_kernel(
+    tc, x_words, x_scales, w1_words, w1_scales, ga, gb, offs, n1, n2, n3, n4, n5, n6, n7, n8, out_0, out_1, out_2
+):
+    nc = tc.nc
+    with ExitStack() as ctx:
+        pool = ctx.enter_context(tc.tile_pool(name="sbuf", bufs=1))
+        psum = ctx.enter_context(tc.psum_pool(name="psum", bufs=1))
+
+        def sb(name, shape, dtype):
+            return pool.tile(shape, dtype, name=name, align_bytes=64)
+
+        def load_list(name, ap):
+            tile = sb(name, list(ap.shape), U16)
+            nc.sync.dma_start(tile[:], ap)
+            return tile
+
+        def load_scale_rows(queue, tile, rows):
+            for q in range(4):
+                queue.dma_start(tile[32 * q : 32 * q + 4, :].bitcast(I32), rows[4 * q : 4 * q + 4, :].bitcast(I32))
+
+        x_sc = sb("x_sc", [P, T], U8)
+        w_sc = sb("w_sc", [P, H], U8)
+        nc.vector.memset(w_sc[:].bitcast(I32), 0)
+        nc.vector.memset(x_sc[:].bitcast(I32), 0)
+
+        w_wd = sb("w_wd", [P, H], U32)
+        x_wd = sb("x_wd", [P, T], U32)
+        l0 = load_list("l0", offs)
+        nc.sync.dma_start(x_wd[:].bitcast(I32), x_words[0].rearrange("p c r -> p (c r)").bitcast(I32))
+        load_scale_rows(nc.scalar, w_sc, w1_scales[0])
+        load_scale_rows(nc.sync, x_sc, x_scales[0])
+        nc.sync.dma_start(w_wd[:].bitcast(I32), w1_words[0].rearrange("p c r -> p (c r)").bitcast(I32))
+        ga_sb = sb("ga_sb", [P, PACK], F32)
+        gb_sb = sb("gb_sb", [P, PACK], F32)
+        nc.sync.dma_start(ga_sb[:], ga.rearrange("(p t) o -> p (t o)", t=PACK))
+        l1 = load_list("l1", n1)
+        l3 = load_list("l3", n3)
+        l2 = load_list("l2", n2)
+        l4 = load_list("l4", n4)
+        l6 = load_list("l6", n6)
+        l5 = load_list("l5", n5)
+        nc.sync.dma_start(gb_sb[:], gb.rearrange("(p t) o -> p (t o)", t=PACK))
+        l7 = load_list("l7", n7)
+        l8 = load_list("l8", n8)
+
+        warm_in = sb("warm_in", [P, 1], F32)
+        warm_out = sb("warm_out", [P, 1], F32)
+        nc.gpsimd.memset(warm_in[:], 0.0)
+        nc.scalar.activation(warm_out[:], warm_in[:], ACT.Sigmoid)
+
+        ga34 = sb("ga34", [P, PACK], F32)
+        nc.scalar.mul(ga34[:], ga_sb[:], 0.75)
+
+        y_win = [sb("y_win%d" % t, [P, WIDE], F32) for t in range(PACK)]
+        ya_win = [sb("ya_win%d" % t, [P, WIDE], F32) for t in range(PACK)]
+        ds = [sb("ds%d" % t, [P, S], F32) for t in range(PACK)]
+        for t in range(PACK):
+            nc.gpsimd.memset(ya_win[t][:, S:], 0.0)
+            nc.gpsimd.memset(y_win[t][:, S:], 0.0)
+
+        xg = sb("xg", [P, S], U32)
+        xsg = sb("xsg", [P, S], U8)
+        w_deal = sb("w_deal", [P, PACK, P], U32)
+        w_sdeal = sb("w_sdeal", [P, PACK, P], U8)
+
+        def deal_words(planes):
+            nc.vector.tensor_copy(
+                w_deal[:].bitcast(I32).rearrange("p t (c i) -> p c t i", i=4)[:, :, planes, :],
+                w_wd[:].bitcast(I32).rearrange("p (c i t) -> p c t i", i=4, t=PACK)[:, :, planes, :],
+            )
+
+        nc.vector.tensor_copy(w_sdeal[:], w_sc[:].rearrange("p (m t) -> p t m", t=PACK))
+        halves = [(slice(h * HALF, (h + 1) * HALF), l0[:, h * HALF // 16 : (h + 1) * HALF // 16]) for h in range(2)]
+        for cols, offsets in halves:
+            nc.vector.tensor_copy(xg[:, cols], x_wd[:].indirect(offsets))
+        deal_words(slice(0, 1))
+        for cols, offsets in halves:
+            nc.vector.tensor_copy(xsg[:, cols], x_sc[:].indirect(offsets))
+        deal_words(slice(1, PACK))
+
+        def project(bank, t, cols):
+            nc.tensor.matmul_mx(
+                out=bank, lhsT=w_deal[:, t, :].bitcast(FP8X4), lhsT_scale=w_sdeal[:, t, :],
+                rhs=xg[:, cols].bitcast(FP8X4), rhs_scale=xsg[:, cols], start=True, stop=True,
+            )
+
+        y_pieces = []
+        for t in range(PACK):
+            if t == 0:
+                spans = [slice(0, HALF), slice(HALF, S)]
+            else:
+                spans = [slice(0, S)]
+            pieces = []
+            for j, cols in enumerate(spans):
+                bank = psum.tile([P, cols.stop - cols.start], F32, name="y_ps%d_%d" % (t, j), tag="bank%d" % (t + j if t == 0 else t + 1))
+                project(bank[:], t, cols)
+                pieces.append((bank, cols))
+            y_pieces.append(pieces)
+
+        sig_b = sb("sig_b", [P, PACK, W], F32)
+        pa = sb("pa", [P, PACK, W], F32)
+        ya1 = sb("ya1", [P, PACK, S], F32)
+        ya3 = sb("ya3", [P, PACK, S], F32)
+        p12 = sb("p12", [P, PACK, S], F32)
+        p34 = sb("p34", [P, PACK, S], F32)
+        z2_bf = sb("z2_bf", [P, S, PACK], BF16)
+
+        def leave_scaled(t):
+            for bank, cols in y_pieces[t]:
+                nc.scalar.activation(ya_win[t][:, cols], bank[:], ACT.Copy, scale=ga34[:, t : t + 1])
+
+        def leave_plain(t):
+            for bank, cols in y_pieces[t]:
+                nc.scalar.copy(y_win[t][:, cols], bank[:])
+            nc.scalar.activation(sig_b[:, t, :], y_win[t][:].indirect(l6[:]), ACT.Sigmoid)
+            for bank, cols in y_pieces[t]:
+                nc.scalar.copy(ds[t][:, cols], bank[:])
+
+        def fetch1(t):
+            nc.vector.tensor_copy(ya1[:, t, :], ya_win[t][:].indirect(l1[:]))
+
+        def fetch3(t):
+            nc.vector.tensor_copy(ya3[:, t, :], ya_win[t][:].indirect(l3[:]))
+
+        def times2(t):
+            nc.vector.tensor_tensor(p12[:, t, :], y_win[t][:].indirect(l2[:]), ya1[:, t, :], ALU.mult)
+
+        def times4(t):
+            nc.vector.tensor_tensor(p34[:, t, :], y_win[t][:].indirect(l4[:]), ya3[:, t, :], ALU.mult)
+
+        def fetch5(t):
+            nc.vector.tensor_copy(pa[:, t, :], y_win[t][:].indirect(l5[:]))
+
+        def put6(t):
+            nc.vector.tensor_tensor(ds[t][:].indirect(l6[:]), pa[:, t, :], sig_b[:, t, :], ALU.mult)
+            nc.scalar.activation(z2_bf[:, :, t], ds[t][:], ACT.Copy, scale=gb_sb[:, t : t + 1])
+
+        leave_scaled(0)
+        leave_plain(0)
+        for t in range(1, PACK):
+            leave_plain(t)
+            leave_scaled(t)
+
+        fetch1(0)
+        fetch3(0)
+        for t in range(PACK):
+            fetch5(t)
+            if t == 0:
+                times2(0)
+            elif t == 1:
+                times4(0)
+            elif t == 2:
+                fetch1(1)
+            else:
+                fetch3(1)
+            put6(t)
+        times2(1)
+        times4(1)
+        for t in range(2, PACK):
+            fetch1(t)
+            fetch3(t)
+            times2(t)
+            times4(t)
+
+        z2_wd = sb("z2_wd", [P, S], U32)
+        z2_sc = sb("z2_sc", [P, S], U8)
+        nc.vector.quantize_mx(out=z2_wd[:].bitcast(FP8X4), scales=z2_sc[:], in_=z2_bf[:].rearrange("p c t -> p (c t)"))
+
+        z_bf = sb("z_bf", [P, PACK, P, PACK], BF16)
+        nc.vector.tensor_tensor(
+            z_bf[:].rearrange("p i m t -> p m t i"),
+            p12[:].rearrange("p t (m i) -> p m t i", i=PACK),
+            p34[:].rearrange("p t (m i) -> p m t i", i=PACK),
+            ALU.subtract,
+        )
+        z_wd = sb("z_wd", [P, PACK, P], U32)
+        z_sc = sb("z_sc", [P, PACK, P], U8)
+
+        s_ps = [[None, None], [None, None]]
+        for h in range(2):
+            for u in range(2):
+                s_ps[h][u] = psum.tile([P, 2, HALF], F32, name="s_ps%d_%d" % (h, u), tag="bank%d" % ((5 + 2 * u + h) % 8))
+        s_win = [sb("s_win%d" % t, [P, S], F32) for t in range(PACK)]
+        for t in range(PACK):
+            nc.vector.quantize_mx(
+                out=z_wd[:, t, :].bitcast(FP8X4), scales=z_sc[:, t, :], in_=z_bf[:, t, :, :].rearrange("p m t -> p (m t)")
+            )
+        for t in range(PACK):
+            for h in range(2):
+                cols = slice(h * HALF, (h + 1) * HALF)
+                region = s_ps[h][t // 2][:, t % 2, :]
+                nc.tensor.matmul_mx(
+                    out=region, lhsT=z_wd[:, t, :].bitcast(FP8X4), lhsT_scale=z_sc[:, t, :],
+                    rhs=z2_wd[:, cols].bitcast(FP8X4), rhs_scale=z2_sc[:, cols], start=True, stop=True,
+                )
+                if t == 0 and h == 1:
+                    nc.vector.tensor_scalar(s_win[t][:, cols], region, 0.0625, None, ALU.mult)
+                else:
+                    nc.scalar.mul(s_win[t][:, cols], region, 0.0625)
+
+        o_wd = sb("o_wd", [P, S], U32)
+        o_sc = sb("o_sc", [P, S], U8)
+        out_rows = out_0.rearrange("(p t) c -> p t c", t=PACK)
+        out_words = out_1[0].rearrange("p c r -> p (c r)").bitcast(I32)
+        for j, (c0, width) in enumerate(PARTS):
+            cols = slice(c0, c0 + width)
+            entries = slice(c0 // 16, (c0 + width) // 16)
+            h = c0 // HALF
+            gate = sb("gate%d" % j, [P, PACK, width], F32)
+            other = sb("other%d" % j, [P, PACK, width], F32)
+            gated = sb("gated%d" % j, [P, PACK, width], F32)
+            best = sb("best%d" % j, [P, PACK, width], F32)
+            best_bf = sb("best_bf%d" % j, [P, width, PACK], BF16)
+            for t in range(PACK):
+                nc.scalar.activation(gate[:, t, :], s_win[t][:].indirect(l7[:, entries]), ACT.Sigmoid)
+                nc.vector.tensor_copy(other[:, t, :], s_win[t][:].indirect(l8[:, entries]))
+            for u in range(2):
+                nc.vector.scalar_tensor_tensor(
+                    gated[:, 2 * u : 2 * u + 2, :], s_ps[h][u][:, :, c0 - h * HALF : c0 - h * HALF + width], 0.0625,
+                    gate[:, 2 * u : 2 * u + 2, :], ALU.mult, ALU.mult,
+                )
+            nc.vector.tensor_tensor(best[:], gated[:], other[:], ALU.max)
+            nc.sync.dma_start(out_rows[:, :, cols], best[:])
+            dst = best_bf[:].rearrange("p (c i) t -> p c t i", i=4)
+            src = best[:].rearrange("p t (c i) -> p c t i", i=4)
+            if j == len(PARTS) - 1:
+                nc.vector.tensor_copy(dst, src)
+            else:
+                nc.scalar.copy(dst, src)
+            nc.vector.quantize_mx(
+                out=o_wd[:, cols].bitcast(FP8X4), scales=o_sc[:, cols], in_=best_bf[:].rearrange("p c t -> p (c t)")
+            )
+            nc.sync.dma_start(out_words[:, cols], o_wd[:, cols].bitcast(I32))
+        for q in range(4):
+            queue = nc.scalar if q % 2 else nc.sync
+            queue.dma_start(out_2[0, 4 * q : 4 * q + 4, :].bitcast(I32), o_sc[32 * q : 32 * q + 4, :].bitcast(I32))

@@ -1,6 +1,7 @@
 from contextlib import ExitStack
 
 import concourse.mybir as mybir
+from concourse.masks import make_identity
 
 K, T, S, H, W = 512, 2048, 512, 512, 256
 FLOPS = 2 * K * H * S + 2 * H * S * S
@@ -30,8 +31,8 @@ def tile_picked_selfdetfoldgmax_none_po_kernel(
         pool = ctx.enter_context(tc.tile_pool(name="sbuf", bufs=1))
         psum = ctx.enter_context(tc.psum_pool(name="psum", bufs=1))
 
-        def sb(name, shape, dtype):
-            return pool.tile(shape, dtype, name=name, align_bytes=64)
+        def sb(name, shape, dtype, tag=None):
+            return pool.tile(shape, dtype, name=name, tag=tag or name, align_bytes=64)
 
         def load_list(name, ap):
             tile = sb(name, list(ap.shape), U16)
@@ -44,19 +45,19 @@ def tile_picked_selfdetfoldgmax_none_po_kernel(
 
         x_sc = sb("x_sc", [P, T], U8)
         w_sc = sb("w_sc", [P, H], U8)
-        nc.vector.memset(w_sc[:].bitcast(I32), 0)
-        nc.vector.memset(x_sc[:].bitcast(I32), 0)
+        nc.gpsimd.memset(w_sc[:].bitcast(I32), 0)
+        nc.gpsimd.memset(x_sc[:].bitcast(I32), 0)
 
         w_wd = sb("w_wd", [P, H], U32)
         x_wd = sb("x_wd", [P, T], U32)
         l0 = load_list("l0", offs)
-        nc.sync.dma_start(x_wd[:].bitcast(I32), x_words[0].rearrange("p c r -> p (c r)").bitcast(I32))
         load_scale_rows(nc.scalar, w_sc, w1_scales[0])
-        load_scale_rows(nc.sync, x_sc, x_scales[0])
+        load_scale_rows(nc.scalar, x_sc, x_scales[0])
         nc.sync.dma_start(w_wd[:].bitcast(I32), w1_words[0].rearrange("p c r -> p (c r)").bitcast(I32))
         ga_sb = sb("ga_sb", [P, PACK], F32)
         gb_sb = sb("gb_sb", [P, PACK], F32)
         nc.sync.dma_start(ga_sb[:], ga.rearrange("(p t) o -> p (t o)", t=PACK))
+        nc.sync.dma_start(x_wd[:].bitcast(I32), x_words[0].rearrange("p c r -> p (c r)").bitcast(I32))
         l1 = load_list("l1", n1)
         l3 = load_list("l3", n3)
         l2 = load_list("l2", n2)
@@ -72,15 +73,14 @@ def tile_picked_selfdetfoldgmax_none_po_kernel(
         nc.gpsimd.memset(warm_in[:], 0.0)
         nc.scalar.activation(warm_out[:], warm_in[:], ACT.Sigmoid)
 
-        ga34 = sb("ga34", [P, PACK], F32)
-        nc.scalar.mul(ga34[:], ga_sb[:], 0.75)
-
         y_win = [sb("y_win%d" % t, [P, WIDE], F32) for t in range(PACK)]
         ya_win = [sb("ya_win%d" % t, [P, WIDE], F32) for t in range(PACK)]
         ds = [sb("ds%d" % t, [P, S], F32) for t in range(PACK)]
         for t in range(PACK):
             nc.gpsimd.memset(ya_win[t][:, S:], 0.0)
             nc.gpsimd.memset(y_win[t][:, S:], 0.0)
+        ident = sb("ident", [P, P], F32)
+        make_identity(nc, ident[:])
 
         xg = sb("xg", [P, S], U32)
         xsg = sb("xsg", [P, S], U8)
@@ -95,12 +95,11 @@ def tile_picked_selfdetfoldgmax_none_po_kernel(
 
         nc.vector.tensor_copy(w_sdeal[:], w_sc[:].rearrange("p (m t) -> p t m", t=PACK))
         halves = [(slice(h * HALF, (h + 1) * HALF), l0[:, h * HALF // 16 : (h + 1) * HALF // 16]) for h in range(2)]
+        deal_words(slice(0, PACK))
         for cols, offsets in halves:
             nc.vector.tensor_copy(xg[:, cols], x_wd[:].indirect(offsets))
-        deal_words(slice(0, 1))
         for cols, offsets in halves:
             nc.vector.tensor_copy(xsg[:, cols], x_sc[:].indirect(offsets))
-        deal_words(slice(1, PACK))
 
         def project(bank, t, cols):
             nc.tensor.matmul_mx(
@@ -127,123 +126,114 @@ def tile_picked_selfdetfoldgmax_none_po_kernel(
         ya3 = sb("ya3", [P, PACK, S], F32)
         p12 = sb("p12", [P, PACK, S], F32)
         p34 = sb("p34", [P, PACK, S], F32)
-        z2_bf = sb("z2_bf", [P, S, PACK], BF16)
+        z_bf = sb("z_bf", [P, PACK, P, 2], F32)
 
-        def leave_scaled(t):
+        for t in range(PACK):
             for bank, cols in y_pieces[t]:
-                nc.scalar.activation(ya_win[t][:, cols], bank[:], ACT.Copy, scale=ga34[:, t : t + 1])
-
-        def leave_plain(t):
+                nc.scalar.activation(ya_win[t][:, cols], bank[:], ACT.Copy, scale=ga_sb[:, t : t + 1])
             for bank, cols in y_pieces[t]:
                 nc.scalar.copy(y_win[t][:, cols], bank[:])
-            nc.scalar.activation(sig_b[:, t, :], y_win[t][:].indirect(l6[:]), ACT.Sigmoid)
+        for t in range(PACK):
             for bank, cols in y_pieces[t]:
                 nc.scalar.copy(ds[t][:, cols], bank[:])
+            nc.scalar.activation(sig_b[:, t, :], y_win[t][:].indirect(l6[:]), ACT.Sigmoid)
 
-        def fetch1(t):
-            nc.vector.tensor_copy(ya1[:, t, :], ya_win[t][:].indirect(l1[:]))
+        zt_banks = (("bank5", "bank6"), ("bank7", "bank0"))
+        back = [psum.tile([P, 2, 2, P], F32, name="back%d" % g, tag="bank%d" % (1 + g)) for g in range(2)]
+        for u in range(2):
+            zt_ps = [psum.tile([P, 2, 2, P], F32, name="zt_ps%d_%d" % (u, g), tag=zt_banks[u][g]) for g in range(2)]
+            for e in range(2):
+                t = 2 * u + e
+                nc.vector.tensor_scalar(ya1[:, t, :], ya_win[t][:].indirect(l1[:]), 0.75, 0.0, ALU.mult, ALU.add)
+                nc.vector.tensor_scalar(ya3[:, t, :], ya_win[t][:].indirect(l3[:]), -0.75, 0.0, ALU.mult, ALU.add)
+                nc.vector.tensor_tensor(p12[:, t, :], y_win[t][:].indirect(l2[:]), ya1[:, t, :], ALU.mult)
+                nc.vector.tensor_tensor(p34[:, t, :], y_win[t][:].indirect(l4[:]), ya3[:, t, :], ALU.mult)
+                for c in range(PACK):
+                    cols = slice(c * P, (c + 1) * P)
+                    region = zt_ps[c // 2][:, e, c % 2, :]
+                    nc.tensor.matmul(region, p12[:, t, cols], ident[:], start=True, stop=False, is_transpose=True)
+                    nc.tensor.matmul(region, p34[:, t, cols], ident[:], start=False, stop=True, is_transpose=True)
+            for g in range(2):
+                zt_bf = sb("zt_bf%d_%d" % (u, g), [P, 2, P, 2], BF16)
+                nc.scalar.copy(zt_bf[:], zt_ps[g][:].rearrange("q e c p -> q c p e"))
+                for c in range(2):
+                    nc.tensor.transpose(back[g][:, c, u, :], zt_bf[:, c, :, :].rearrange("q p e -> q (p e)").bitcast(F32), ident[:])
+        for g in range(2):
+            nc.scalar.copy(
+                z_bf[:, :, 64 * g : 64 * (g + 1), :].rearrange("p i (c m) u -> p i c m u", c=2),
+                back[g][:].rearrange("p c u (m i) -> p i c m u", i=PACK),
+            )
 
-        def fetch3(t):
-            nc.vector.tensor_copy(ya3[:, t, :], ya_win[t][:].indirect(l3[:]))
-
-        def times2(t):
-            nc.vector.tensor_tensor(p12[:, t, :], y_win[t][:].indirect(l2[:]), ya1[:, t, :], ALU.mult)
-
-        def times4(t):
-            nc.vector.tensor_tensor(p34[:, t, :], y_win[t][:].indirect(l4[:]), ya3[:, t, :], ALU.mult)
+        z2_bf = [sb("z2_bf%d" % h, [P, HALF, PACK], BF16, tag="zt_bf1_%d" % h) for h in range(2)]
 
         def fetch5(t):
             nc.vector.tensor_copy(pa[:, t, :], y_win[t][:].indirect(l5[:]))
 
         def put6(t):
             nc.vector.tensor_tensor(ds[t][:].indirect(l6[:]), pa[:, t, :], sig_b[:, t, :], ALU.mult)
-            nc.scalar.activation(z2_bf[:, :, t], ds[t][:], ACT.Copy, scale=gb_sb[:, t : t + 1])
+            for h in range(2):
+                nc.scalar.activation(z2_bf[h][:, :, t], ds[t][:, h * HALF : (h + 1) * HALF], ACT.Copy, scale=gb_sb[:, t : t + 1])
 
-        leave_scaled(0)
-        leave_plain(0)
-        for t in range(1, PACK):
-            leave_plain(t)
-            leave_scaled(t)
-
-        fetch1(0)
-        fetch3(0)
+        fetch5(0)
         for t in range(PACK):
-            fetch5(t)
-            if t == 0:
-                times2(0)
-            elif t == 1:
-                times4(0)
-            elif t == 2:
-                fetch1(1)
-            else:
-                fetch3(1)
+            if t + 1 < PACK:
+                fetch5(t + 1)
             put6(t)
-        times2(1)
-        times4(1)
-        for t in range(2, PACK):
-            fetch1(t)
-            fetch3(t)
-            times2(t)
-            times4(t)
 
+        z_wd = sb("z_wd", [P, S], U32)
+        z_sc = sb("z_sc", [P, S], U8)
+        nc.vector.quantize_mx(out=z_wd[:].bitcast(FP8X4), scales=z_sc[:], in_=z_bf[:].rearrange("p i m u -> p (i m u)").bitcast(BF16))
         z2_wd = sb("z2_wd", [P, S], U32)
         z2_sc = sb("z2_sc", [P, S], U8)
-        nc.vector.quantize_mx(out=z2_wd[:].bitcast(FP8X4), scales=z2_sc[:], in_=z2_bf[:].rearrange("p c t -> p (c t)"))
-
-        z_bf = sb("z_bf", [P, PACK, P, PACK], BF16)
-        nc.vector.tensor_tensor(
-            z_bf[:].rearrange("p i m t -> p m t i"),
-            p12[:].rearrange("p t (m i) -> p m t i", i=PACK),
-            p34[:].rearrange("p t (m i) -> p m t i", i=PACK),
-            ALU.subtract,
-        )
-        z_wd = sb("z_wd", [P, PACK, P], U32)
-        z_sc = sb("z_sc", [P, PACK, P], U8)
+        for h in range(2):
+            cols = slice(h * HALF, (h + 1) * HALF)
+            nc.vector.quantize_mx(
+                out=z2_wd[:, cols].bitcast(FP8X4), scales=z2_sc[:, cols], in_=z2_bf[h][:].rearrange("p c t -> p (c t)")
+            )
 
         s_ps = [[None, None], [None, None]]
         for h in range(2):
             for u in range(2):
-                s_ps[h][u] = psum.tile([P, 2, HALF], F32, name="s_ps%d_%d" % (h, u), tag="bank%d" % ((5 + 2 * u + h) % 8))
-        s_win = [sb("s_win%d" % t, [P, S], F32) for t in range(PACK)]
+                s_ps[h][u] = psum.tile([P, 2, HALF], F32, name="s_ps%d_%d" % (h, u), tag="bank%d" % (3 + 2 * u + h))
+        s_win = y_win
+        gate = [sb("gate%d" % h, [P, PACK, HALF], F32) for h in range(2)]
+        other = sb("other", [P, PACK, S], F32)
         for t in range(PACK):
-            nc.vector.quantize_mx(
-                out=z_wd[:, t, :].bitcast(FP8X4), scales=z_sc[:, t, :], in_=z_bf[:, t, :, :].rearrange("p m t -> p (m t)")
-            )
-        for t in range(PACK):
+            rows = slice(t * P, (t + 1) * P)
             for h in range(2):
                 cols = slice(h * HALF, (h + 1) * HALF)
                 region = s_ps[h][t // 2][:, t % 2, :]
                 nc.tensor.matmul_mx(
-                    out=region, lhsT=z_wd[:, t, :].bitcast(FP8X4), lhsT_scale=z_sc[:, t, :],
+                    out=region, lhsT=z_wd[:, rows].bitcast(FP8X4), lhsT_scale=z_sc[:, rows],
                     rhs=z2_wd[:, cols].bitcast(FP8X4), rhs_scale=z2_sc[:, cols], start=True, stop=True,
                 )
                 if t == 0 and h == 1:
                     nc.vector.tensor_scalar(s_win[t][:, cols], region, 0.0625, None, ALU.mult)
                 else:
                     nc.scalar.mul(s_win[t][:, cols], region, 0.0625)
+            nc.vector.tensor_copy(other[:, t, :], s_win[t][:].indirect(l8[:]))
+        for h in range(2):
+            for t in range(PACK):
+                nc.scalar.activation(gate[h][:, t, :], s_win[t][:].indirect(l7[:, h * HALF // 16 : (h + 1) * HALF // 16]), ACT.Sigmoid)
 
         o_wd = sb("o_wd", [P, S], U32)
         o_sc = sb("o_sc", [P, S], U8)
         out_rows = out_0.rearrange("(p t) c -> p t c", t=PACK)
         out_words = out_1[0].rearrange("p c r -> p (c r)").bitcast(I32)
+        finished = []
         for j, (c0, width) in enumerate(PARTS):
             cols = slice(c0, c0 + width)
-            entries = slice(c0 // 16, (c0 + width) // 16)
             h = c0 // HALF
-            gate = sb("gate%d" % j, [P, PACK, width], F32)
-            other = sb("other%d" % j, [P, PACK, width], F32)
+            within = slice(c0 - h * HALF, c0 - h * HALF + width)
             gated = sb("gated%d" % j, [P, PACK, width], F32)
             best = sb("best%d" % j, [P, PACK, width], F32)
             best_bf = sb("best_bf%d" % j, [P, width, PACK], BF16)
-            for t in range(PACK):
-                nc.scalar.activation(gate[:, t, :], s_win[t][:].indirect(l7[:, entries]), ACT.Sigmoid)
-                nc.vector.tensor_copy(other[:, t, :], s_win[t][:].indirect(l8[:, entries]))
             for u in range(2):
                 nc.vector.scalar_tensor_tensor(
-                    gated[:, 2 * u : 2 * u + 2, :], s_ps[h][u][:, :, c0 - h * HALF : c0 - h * HALF + width], 0.0625,
-                    gate[:, 2 * u : 2 * u + 2, :], ALU.mult, ALU.mult,
+                    gated[:, 2 * u : 2 * u + 2, :], s_ps[h][u][:, :, within], 0.0625,
+                    gate[h][:, 2 * u : 2 * u + 2, within], ALU.mult, ALU.mult,
                 )
-            nc.vector.tensor_tensor(best[:], gated[:], other[:], ALU.max)
+            nc.vector.tensor_tensor(best[:], gated[:], other[:, :, cols], ALU.max)
             nc.sync.dma_start(out_rows[:, :, cols], best[:])
             dst = best_bf[:].rearrange("p (c i) t -> p c t i", i=4)
             src = best[:].rearrange("p t (c i) -> p c t i", i=4)
@@ -251,6 +241,8 @@ def tile_picked_selfdetfoldgmax_none_po_kernel(
                 nc.vector.tensor_copy(dst, src)
             else:
                 nc.scalar.copy(dst, src)
+            finished.append((cols, best_bf))
+        for cols, best_bf in finished:
             nc.vector.quantize_mx(
                 out=o_wd[:, cols].bitcast(FP8X4), scales=o_sc[:, cols], in_=best_bf[:].rearrange("p c t -> p (c t)")
             )

@@ -77,8 +77,9 @@ def tile_picked_selfdetfoldgmax_none_po_kernel(
         ya_win = [sb("ya_win%d" % t, [P, WIDE], F32) for t in range(PACK)]
         ds = [sb("ds%d" % t, [P, S], F32) for t in range(PACK)]
         for t in range(PACK):
-            nc.gpsimd.memset(ya_win[t][:, S:], 0.0)
-            nc.gpsimd.memset(y_win[t][:, S:], 0.0)
+            engine = nc.vector if t < 2 else nc.gpsimd
+            engine.memset(ya_win[t][:, S:], 0.0)
+            engine.memset(y_win[t][:, S:], 0.0)
         ident = sb("ident", [P, P], F32)
         make_identity(nc, ident[:])
 
@@ -220,33 +221,50 @@ def tile_picked_selfdetfoldgmax_none_po_kernel(
         o_sc = sb("o_sc", [P, S], U8)
         out_rows = out_0.rearrange("(p t) c -> p t c", t=PACK)
         out_words = out_1[0].rearrange("p c r -> p (c r)").bitcast(I32)
-        finished = []
-        for j, (c0, width) in enumerate(PARTS):
-            cols = slice(c0, c0 + width)
+        gated = [sb("gated%d" % h, [P, PACK, HALF], F32) for h in range(2)]
+        best = [sb("best%d" % j, [P, PACK, width], F32) for j, (c0, width) in enumerate(PARTS)]
+        best_bf = [sb("best_bf%d" % j, [P, width, PACK], BF16) for j, (c0, width) in enumerate(PARTS)]
+
+        def apply_gate(h, u):
+            planes = slice(2 * u, 2 * u + 2)
+            nc.vector.scalar_tensor_tensor(gated[h][:, planes, :], s_ps[h][u][:], 0.0625, gate[h][:, planes, :], ALU.mult, ALU.mult)
+
+        def take_larger(j):
+            c0, width = PARTS[j]
             h = c0 // HALF
-            within = slice(c0 - h * HALF, c0 - h * HALF + width)
-            gated = sb("gated%d" % j, [P, PACK, width], F32)
-            best = sb("best%d" % j, [P, PACK, width], F32)
-            best_bf = sb("best_bf%d" % j, [P, width, PACK], BF16)
-            for u in range(2):
-                nc.vector.scalar_tensor_tensor(
-                    gated[:, 2 * u : 2 * u + 2, :], s_ps[h][u][:, :, within], 0.0625,
-                    gate[h][:, 2 * u : 2 * u + 2, within], ALU.mult, ALU.mult,
-                )
-            nc.vector.tensor_tensor(best[:], gated[:], other[:, :, cols], ALU.max)
-            nc.sync.dma_start(out_rows[:, :, cols], best[:])
-            dst = best_bf[:].rearrange("p (c i) t -> p c t i", i=4)
-            src = best[:].rearrange("p t (c i) -> p c t i", i=4)
-            if j == len(PARTS) - 1:
-                nc.vector.tensor_copy(dst, src)
-            else:
-                nc.scalar.copy(dst, src)
-            finished.append((cols, best_bf))
-        for cols, best_bf in finished:
-            nc.vector.quantize_mx(
-                out=o_wd[:, cols].bitcast(FP8X4), scales=o_sc[:, cols], in_=best_bf[:].rearrange("p c t -> p (c t)")
+            nc.vector.tensor_tensor(
+                best[j][:], gated[h][:, :, c0 - h * HALF : c0 - h * HALF + width], other[:, :, c0 : c0 + width], ALU.max
             )
+            nc.sync.dma_start(out_rows[:, :, c0 : c0 + width], best[j][:])
+
+        def weave(j, copy):
+            copy(best_bf[j][:].rearrange("p (c i) t -> p c t i", i=4), best[j][:].rearrange("p t (c i) -> p c t i", i=4))
+
+        def quantize_out(j):
+            c0, width = PARTS[j]
+            cols = slice(c0, c0 + width)
+            nc.vector.quantize_mx(
+                out=o_wd[:, cols].bitcast(FP8X4), scales=o_sc[:, cols], in_=best_bf[j][:].rearrange("p c t -> p (c t)")
+            )
+
+        def store_words(cols):
             nc.sync.dma_start(out_words[:, cols], o_wd[:, cols].bitcast(I32))
+
+        apply_gate(0, 0)
+        apply_gate(0, 1)
+        apply_gate(1, 0)
+        take_larger(0)
+        weave(0, nc.scalar.copy)
+        apply_gate(1, 1)
+        take_larger(1)
+        weave(1, nc.scalar.copy)
+        take_larger(2)
+        quantize_out(0)
+        weave(2, nc.vector.tensor_copy)
+        quantize_out(1)
+        store_words(slice(0, PARTS[2][0]))
+        quantize_out(2)
+        store_words(slice(PARTS[2][0], S))
         for q in range(4):
             queue = nc.scalar if q % 2 else nc.sync
             queue.dma_start(out_2[0, 4 * q : 4 * q + 4, :].bitcast(I32), o_sc[32 * q : 32 * q + 4, :].bitcast(I32))

@@ -199,6 +199,15 @@ def tile_picked_selfdetfoldgmax_none_po_kernel(
         s_win = y_win
         gate = [sb("gate%d" % h, [P, PACK, HALF], F32) for h in range(2)]
         other = sb("other", [P, PACK, S], F32)
+        gated = [sb("gated%d" % h, [P, PACK, HALF], F32) for h in range(2)]
+
+        def fetch_gate(h, t):
+            nc.scalar.activation(gate[h][:, t, :], s_win[t][:].indirect(l7[:, h * HALF // 16 : (h + 1) * HALF // 16]), ACT.Sigmoid)
+
+        def first_half_gate(t):
+            fetch_gate(0, t)
+            nc.gpsimd.tensor_tensor(gated[0][:, t, :], s_win[t][:, :HALF], gate[0][:, t, :], ALU.mult)
+
         for t in range(PACK):
             rows = slice(t * P, (t + 1) * P)
             for h in range(2):
@@ -213,15 +222,16 @@ def tile_picked_selfdetfoldgmax_none_po_kernel(
                 else:
                     nc.scalar.mul(s_win[t][:, cols], region, 0.0625)
             nc.vector.tensor_copy(other[:, t, :], s_win[t][:].indirect(l8[:]))
-        for h in range(2):
-            for t in range(PACK):
-                nc.scalar.activation(gate[h][:, t, :], s_win[t][:].indirect(l7[:, h * HALF // 16 : (h + 1) * HALF // 16]), ACT.Sigmoid)
+            if t > 0:
+                first_half_gate(t - 1)
+        first_half_gate(PACK - 1)
+        for t in range(PACK):
+            fetch_gate(1, t)
 
         o_wd = sb("o_wd", [P, S], U32)
         o_sc = sb("o_sc", [P, S], U8)
         out_rows = out_0.rearrange("(p t) c -> p t c", t=PACK)
         out_words = out_1[0].rearrange("p c r -> p (c r)").bitcast(I32)
-        gated = [sb("gated%d" % h, [P, PACK, HALF], F32) for h in range(2)]
         best = [sb("best%d" % j, [P, PACK, width], F32) for j, (c0, width) in enumerate(PARTS)]
         best_bf = [sb("best_bf%d" % j, [P, width, PACK], BF16) for j, (c0, width) in enumerate(PARTS)]
 
@@ -232,9 +242,11 @@ def tile_picked_selfdetfoldgmax_none_po_kernel(
         def take_larger(j):
             c0, width = PARTS[j]
             h = c0 // HALF
-            nc.vector.tensor_tensor(
-                best[j][:], gated[h][:, :, c0 - h * HALF : c0 - h * HALF + width], other[:, :, c0 : c0 + width], ALU.max
-            )
+            for planes in (slice(0, 2), slice(2, 4)) if j == 0 else (slice(0, 4),):
+                nc.vector.tensor_tensor(
+                    best[j][:, planes, :], gated[h][:, planes, c0 - h * HALF : c0 - h * HALF + width],
+                    other[:, planes, c0 : c0 + width], ALU.max,
+                )
             nc.sync.dma_start(out_rows[:, :, c0 : c0 + width], best[j][:])
 
         def weave(j, copy):
@@ -250,11 +262,9 @@ def tile_picked_selfdetfoldgmax_none_po_kernel(
         def store_words(cols):
             nc.sync.dma_start(out_words[:, cols], o_wd[:, cols].bitcast(I32))
 
-        apply_gate(0, 0)
-        apply_gate(0, 1)
-        apply_gate(1, 0)
         take_larger(0)
         weave(0, nc.scalar.copy)
+        apply_gate(1, 0)
         apply_gate(1, 1)
         take_larger(1)
         weave(1, nc.scalar.copy)

@@ -20,6 +20,7 @@ P = 128
 PACK = 4
 HALF = S // 2
 WIDE = 2 * S
+HALVES = ((0, HALF), (HALF, HALF))
 PARTS = ((0, 256), (256, 128), (384, 128))
 
 
@@ -165,15 +166,22 @@ def tile_picked_selfdetfoldgmax_none_po_kernel(
                 back[g][:].rearrange("p c u (m i) -> p i c m u", i=PACK),
             )
 
-        z2_bf = [sb("z2_bf%d" % h, [P, HALF, PACK], BF16, tag="zt_bf1_%d" % h) for h in range(2)]
+        z2_bf = [sb("z2_bf%d" % h, [P, HALF * PACK], BF16, tag="zt_bf1_%d" % h) for h in range(2)]
+
+        def z2_run(c0, width):
+            h = c0 // HALF
+            return z2_bf[h][:, (c0 - h * HALF) * PACK : (c0 - h * HALF + width) * PACK]
+
+        def z2_cols(c0, width):
+            return z2_run(c0, width).rearrange("p (c t) -> p c t", t=PACK)
 
         def fetch5(t):
             nc.vector.tensor_copy(pa[:, t, :], y_win[t][:].indirect(l5[:]))
 
         def put6(t):
             nc.vector.tensor_tensor(ds[t][:].indirect(l6[:]), pa[:, t, :], sig_b[:, t, :], ALU.mult)
-            for h in range(2):
-                nc.scalar.activation(z2_bf[h][:, :, t], ds[t][:, h * HALF : (h + 1) * HALF], ACT.Copy, scale=gb_sb[:, t : t + 1])
+            for c0, width in PARTS if t == PACK - 1 else HALVES:
+                nc.scalar.activation(z2_cols(c0, width)[:, :, t], ds[t][:, c0 : c0 + width], ACT.Copy, scale=gb_sb[:, t : t + 1])
 
         fetch5(0)
         for t in range(PACK):
@@ -186,11 +194,9 @@ def tile_picked_selfdetfoldgmax_none_po_kernel(
         nc.vector.quantize_mx(out=z_wd[:].bitcast(FP8X4), scales=z_sc[:], in_=z_bf[:].rearrange("p i m u -> p (i m u)").bitcast(BF16))
         z2_wd = sb("z2_wd", [P, S], U32)
         z2_sc = sb("z2_sc", [P, S], U8)
-        for h in range(2):
-            cols = slice(h * HALF, (h + 1) * HALF)
-            nc.vector.quantize_mx(
-                out=z2_wd[:, cols].bitcast(FP8X4), scales=z2_sc[:, cols], in_=z2_bf[h][:].rearrange("p c t -> p (c t)")
-            )
+        for c0, width in PARTS:
+            cols = slice(c0, c0 + width)
+            nc.vector.quantize_mx(out=z2_wd[:, cols].bitcast(FP8X4), scales=z2_sc[:, cols], in_=z2_run(c0, width))
 
         s_ps = [[None, None], [None, None]]
         for h in range(2):
@@ -208,22 +214,36 @@ def tile_picked_selfdetfoldgmax_none_po_kernel(
             fetch_gate(0, t)
             nc.gpsimd.tensor_tensor(gated[0][:, t, :], s_win[t][:, :HALF], gate[0][:, t, :], ALU.mult)
 
-        for t in range(PACK):
+        def similarity(t):
             rows = slice(t * P, (t + 1) * P)
-            for h in range(2):
-                cols = slice(h * HALF, (h + 1) * HALF)
-                region = s_ps[h][t // 2][:, t % 2, :]
+            for c0, width in PARTS if t == 0 else HALVES:
+                h = c0 // HALF
+                cols = slice(c0, c0 + width)
                 nc.tensor.matmul_mx(
-                    out=region, lhsT=z_wd[:, rows].bitcast(FP8X4), lhsT_scale=z_sc[:, rows],
+                    out=s_ps[h][t // 2][:, t % 2, c0 - h * HALF : c0 - h * HALF + width],
+                    lhsT=z_wd[:, rows].bitcast(FP8X4), lhsT_scale=z_sc[:, rows],
                     rhs=z2_wd[:, cols].bitcast(FP8X4), rhs_scale=z2_sc[:, cols], start=True, stop=True,
                 )
-                if t == 0 and h == 1:
-                    nc.vector.tensor_scalar(s_win[t][:, cols], region, 0.0625, None, ALU.mult)
-                else:
-                    nc.scalar.mul(s_win[t][:, cols], region, 0.0625)
+            nc.scalar.mul(s_win[t][:, :HALF], s_ps[0][t // 2][:, t % 2, :], 0.0625)
+            if t % 2 == 0:
+                nc.vector.tensor_scalar(s_win[t][:, HALF:S], s_ps[1][t // 2][:, t % 2, :], 0.0625, None, ALU.mult)
+            else:
+                nc.scalar.mul(s_win[t][:, HALF:S], s_ps[1][t // 2][:, t % 2, :], 0.0625)
+
+        def fetch_other(t):
             nc.vector.tensor_copy(other[:, t, :], s_win[t][:].indirect(l8[:]))
-            if t > 0:
-                first_half_gate(t - 1)
+
+        similarity(0)
+        fetch_other(0)
+        similarity(1)
+        first_half_gate(0)
+        similarity(2)
+        fetch_other(1)
+        fetch_other(2)
+        first_half_gate(1)
+        similarity(3)
+        fetch_other(3)
+        first_half_gate(2)
         first_half_gate(PACK - 1)
         for t in range(PACK):
             fetch_gate(1, t)

from contextlib import ExitStack

import concourse.mybir as mybir
from concourse.masks import make_identity

K, T, S, H, W = 512, 2048, 512, 512, 256
FLOPS = 2 * K * H * S + 2 * H * S * S

F32 = mybir.dt.float32
BF16 = mybir.dt.bfloat16
I32 = mybir.dt.int32
U32 = mybir.dt.uint32
U16 = mybir.dt.uint16
U8 = mybir.dt.uint8
FP8X4 = mybir.dt.float8_e4m3fn_x4
ALU = mybir.AluOpType
ACT = mybir.ActivationFunctionType

P = 128
PACK = 4
HALF = S // 2
WIDE = 2 * S
HALVES = ((0, HALF), (HALF, HALF))
PARTS = ((0, 256), (256, 128), (384, 128))


def tile_picked_selfdetfoldgmax_none_po_kernel(
    tc, x_words, x_scales, w1_words, w1_scales, ga, gb, offs, n1, n2, n3, n4, n5, n6, n7, n8, out_0, out_1, out_2
):
    nc = tc.nc
    with ExitStack() as ctx:
        pool = ctx.enter_context(tc.tile_pool(name="sbuf", bufs=1))
        psum = ctx.enter_context(tc.psum_pool(name="psum", bufs=1))

        def sb(name, shape, dtype, tag=None):
            return pool.tile(shape, dtype, name=name, tag=tag or name, align_bytes=64)

        def load_list(name, ap):
            tile = sb(name, list(ap.shape), U16)
            nc.sync.dma_start(tile[:], ap)
            return tile

        def load_scale_rows(queue, tile, rows):
            for q in range(4):
                queue.dma_start(tile[32 * q : 32 * q + 4, :].bitcast(I32), rows[4 * q : 4 * q + 4, :].bitcast(I32))

        x_sc = sb("x_sc", [P, T], U8)
        w_sc = sb("w_sc", [P, H], U8)
        nc.gpsimd.memset(w_sc[:].bitcast(I32), 0)
        nc.gpsimd.memset(x_sc[:].bitcast(I32), 0)

        w_wd = sb("w_wd", [P, H], U32)
        x_wd = sb("x_wd", [P, T], U32)
        l0 = load_list("l0", offs)
        load_scale_rows(nc.scalar, w_sc, w1_scales[0])
        load_scale_rows(nc.scalar, x_sc, x_scales[0])
        nc.sync.dma_start(w_wd[:].bitcast(I32), w1_words[0].rearrange("p c r -> p (c r)").bitcast(I32))
        ga_sb = sb("ga_sb", [P, PACK], F32)
        gb_sb = sb("gb_sb", [P, PACK], F32)
        nc.sync.dma_start(ga_sb[:], ga.rearrange("(p t) o -> p (t o)", t=PACK))
        nc.sync.dma_start(x_wd[:].bitcast(I32), x_words[0].rearrange("p c r -> p (c r)").bitcast(I32))
        l1 = load_list("l1", n1)
        l3 = load_list("l3", n3)
        l2 = load_list("l2", n2)
        l4 = load_list("l4", n4)
        l6 = load_list("l6", n6)
        l5 = load_list("l5", n5)
        nc.sync.dma_start(gb_sb[:], gb.rearrange("(p t) o -> p (t o)", t=PACK))
        l7 = load_list("l7", n7)
        l8 = load_list("l8", n8)

        warm_in = sb("warm_in", [P, 1], F32)
        warm_out = sb("warm_out", [P, 1], F32)
        nc.gpsimd.memset(warm_in[:], 0.0)
        nc.scalar.activation(warm_out[:], warm_in[:], ACT.Sigmoid)

        y_win = [sb("y_win%d" % t, [P, WIDE], F32) for t in range(PACK)]
        ya_win = [sb("ya_win%d" % t, [P, WIDE], F32) for t in range(PACK)]
        ds = [sb("ds%d" % t, [P, S], F32) for t in range(PACK)]
        for t in range(PACK):
            engine = nc.vector if t < 2 else nc.gpsimd
            engine.memset(ya_win[t][:, S:], 0.0)
            engine.memset(y_win[t][:, S:], 0.0)
        ident = sb("ident", [P, P], F32)
        make_identity(nc, ident[:])

        xg = sb("xg", [P, S], U32)
        xsg = sb("xsg", [P, S], U8)
        w_deal = sb("w_deal", [P, PACK, P], U32)
        w_sdeal = sb("w_sdeal", [P, PACK, P], U8)

        def deal_words(planes):
            nc.vector.tensor_copy(
                w_deal[:].bitcast(I32).rearrange("p t (c i) -> p c t i", i=4)[:, :, planes, :],
                w_wd[:].bitcast(I32).rearrange("p (c i t) -> p c t i", i=4, t=PACK)[:, :, planes, :],
            )

        nc.vector.tensor_copy(w_sdeal[:], w_sc[:].rearrange("p (m t) -> p t m", t=PACK))
        halves = [(slice(h * HALF, (h + 1) * HALF), l0[:, h * HALF // 16 : (h + 1) * HALF // 16]) for h in range(2)]
        deal_words(slice(0, PACK))
        for cols, offsets in halves:
            nc.vector.tensor_copy(xg[:, cols], x_wd[:].indirect(offsets))
        for cols, offsets in halves:
            nc.vector.tensor_copy(xsg[:, cols], x_sc[:].indirect(offsets))

        def project(bank, t, cols):
            nc.tensor.matmul_mx(
                out=bank, lhsT=w_deal[:, t, :].bitcast(FP8X4), lhsT_scale=w_sdeal[:, t, :],
                rhs=xg[:, cols].bitcast(FP8X4), rhs_scale=xsg[:, cols], start=True, stop=True,
            )

        y_pieces = []
        for t in range(PACK):
            if t == 0:
                spans = [slice(0, HALF), slice(HALF, S)]
            else:
                spans = [slice(0, S)]
            pieces = []
            for j, cols in enumerate(spans):
                bank = psum.tile([P, cols.stop - cols.start], F32, name="y_ps%d_%d" % (t, j), tag="bank%d" % (t + j if t == 0 else t + 1))
                project(bank[:], t, cols)
                pieces.append((bank, cols))
            y_pieces.append(pieces)

        sig_b = sb("sig_b", [P, PACK, W], F32)
        pa = sb("pa", [P, PACK, W], F32)
        ya1 = sb("ya1", [P, PACK, S], F32)
        ya3 = sb("ya3", [P, PACK, S], F32)
        p12 = sb("p12", [P, PACK, S], F32)
        p34 = sb("p34", [P, PACK, S], F32)
        z_bf = sb("z_bf", [P, PACK, P, 2], F32)

        for t in range(PACK):
            for bank, cols in y_pieces[t]:
                nc.scalar.activation(ya_win[t][:, cols], bank[:], ACT.Copy, scale=ga_sb[:, t : t + 1])
            for bank, cols in y_pieces[t]:
                nc.scalar.copy(y_win[t][:, cols], bank[:])
        for t in range(PACK):
            for bank, cols in y_pieces[t]:
                nc.scalar.copy(ds[t][:, cols], bank[:])
            nc.scalar.activation(sig_b[:, t, :], y_win[t][:].indirect(l6[:]), ACT.Sigmoid)

        zt_banks = (("bank5", "bank6"), ("bank7", "bank0"))
        back = [psum.tile([P, 2, 2, P], F32, name="back%d" % g, tag="bank%d" % (1 + g)) for g in range(2)]
        for u in range(2):
            zt_ps = [psum.tile([P, 2, 2, P], F32, name="zt_ps%d_%d" % (u, g), tag=zt_banks[u][g]) for g in range(2)]
            for e in range(2):
                t = 2 * u + e
                nc.vector.tensor_scalar(ya1[:, t, :], ya_win[t][:].indirect(l1[:]), 0.75, 0.0, ALU.mult, ALU.add)
                nc.vector.tensor_scalar(ya3[:, t, :], ya_win[t][:].indirect(l3[:]), -0.75, 0.0, ALU.mult, ALU.add)
                nc.vector.tensor_tensor(p12[:, t, :], y_win[t][:].indirect(l2[:]), ya1[:, t, :], ALU.mult)
                nc.vector.tensor_tensor(p34[:, t, :], y_win[t][:].indirect(l4[:]), ya3[:, t, :], ALU.mult)
                for c in range(PACK):
                    cols = slice(c * P, (c + 1) * P)
                    region = zt_ps[c // 2][:, e, c % 2, :]
                    nc.tensor.matmul(region, p12[:, t, cols], ident[:], start=True, stop=False, is_transpose=True)
                    nc.tensor.matmul(region, p34[:, t, cols], ident[:], start=False, stop=True, is_transpose=True)
            for g in range(2):
                zt_bf = sb("zt_bf%d_%d" % (u, g), [P, 2, P, 2], BF16)
                nc.scalar.copy(zt_bf[:], zt_ps[g][:].rearrange("q e c p -> q c p e"))
                for c in range(2):
                    nc.tensor.transpose(back[g][:, c, u, :], zt_bf[:, c, :, :].rearrange("q p e -> q (p e)").bitcast(F32), ident[:])
        for g in range(2):
            nc.scalar.copy(
                z_bf[:, :, 64 * g : 64 * (g + 1), :].rearrange("p i (c m) u -> p i c m u", c=2),
                back[g][:].rearrange("p c u (m i) -> p i c m u", i=PACK),
            )

        z2_bf = [sb("z2_bf%d" % h, [P, HALF * PACK], BF16, tag="zt_bf1_%d" % h) for h in range(2)]

        def z2_run(c0, width):
            h = c0 // HALF
            return z2_bf[h][:, (c0 - h * HALF) * PACK : (c0 - h * HALF + width) * PACK]

        def z2_cols(c0, width):
            return z2_run(c0, width).rearrange("p (c t) -> p c t", t=PACK)

        def fetch5(t):
            nc.vector.tensor_copy(pa[:, t, :], y_win[t][:].indirect(l5[:]))

        def put6(t):
            nc.vector.tensor_tensor(ds[t][:].indirect(l6[:]), pa[:, t, :], sig_b[:, t, :], ALU.mult)
            for c0, width in PARTS if t == PACK - 1 else HALVES:
                nc.scalar.activation(z2_cols(c0, width)[:, :, t], ds[t][:, c0 : c0 + width], ACT.Copy, scale=gb_sb[:, t : t + 1])

        fetch5(0)
        for t in range(PACK):
            if t + 1 < PACK:
                fetch5(t + 1)
            put6(t)

        z_wd = sb("z_wd", [P, S], U32)
        z_sc = sb("z_sc", [P, S], U8)
        nc.vector.quantize_mx(out=z_wd[:].bitcast(FP8X4), scales=z_sc[:], in_=z_bf[:].rearrange("p i m u -> p (i m u)").bitcast(BF16))
        z2_wd = sb("z2_wd", [P, S], U32)
        z2_sc = sb("z2_sc", [P, S], U8)
        for c0, width in PARTS:
            cols = slice(c0, c0 + width)
            nc.vector.quantize_mx(out=z2_wd[:, cols].bitcast(FP8X4), scales=z2_sc[:, cols], in_=z2_run(c0, width))

        s_ps = [[None, None], [None, None]]
        for h in range(2):
            for u in range(2):
                s_ps[h][u] = psum.tile([P, 2, HALF], F32, name="s_ps%d_%d" % (h, u), tag="bank%d" % (3 + 2 * u + h))
        s_win = y_win
        gate = [sb("gate%d" % h, [P, PACK, HALF], F32) for h in range(2)]
        other = sb("other", [P, PACK, S], F32)
        gated = [sb("gated%d" % h, [P, PACK, HALF], F32) for h in range(2)]

        def fetch_gate(h, t):
            nc.scalar.activation(gate[h][:, t, :], s_win[t][:].indirect(l7[:, h * HALF // 16 : (h + 1) * HALF // 16]), ACT.Sigmoid)

        def first_half_gate(t):
            fetch_gate(0, t)
            nc.gpsimd.tensor_tensor(gated[0][:, t, :], s_win[t][:, :HALF], gate[0][:, t, :], ALU.mult)

        def similarity(t):
            rows = slice(t * P, (t + 1) * P)
            for c0, width in PARTS if t == 0 else HALVES:
                h = c0 // HALF
                cols = slice(c0, c0 + width)
                nc.tensor.matmul_mx(
                    out=s_ps[h][t // 2][:, t % 2, c0 - h * HALF : c0 - h * HALF + width],
                    lhsT=z_wd[:, rows].bitcast(FP8X4), lhsT_scale=z_sc[:, rows],
                    rhs=z2_wd[:, cols].bitcast(FP8X4), rhs_scale=z2_sc[:, cols], start=True, stop=True,
                )
            nc.scalar.mul(s_win[t][:, :HALF], s_ps[0][t // 2][:, t % 2, :], 0.0625)
            if t % 2 == 0:
                nc.vector.tensor_scalar(s_win[t][:, HALF:S], s_ps[1][t // 2][:, t % 2, :], 0.0625, None, ALU.mult)
            else:
                nc.scalar.mul(s_win[t][:, HALF:S], s_ps[1][t // 2][:, t % 2, :], 0.0625)

        def fetch_other(t):
            nc.vector.tensor_copy(other[:, t, :], s_win[t][:].indirect(l8[:]))

        similarity(0)
        fetch_other(0)
        similarity(1)
        first_half_gate(0)
        similarity(2)
        fetch_other(1)
        fetch_other(2)
        first_half_gate(1)
        similarity(3)
        fetch_other(3)
        first_half_gate(2)
        first_half_gate(PACK - 1)
        for t in range(PACK):
            fetch_gate(1, t)

        o_wd = sb("o_wd", [P, S], U32)
        o_sc = sb("o_sc", [P, S], U8)
        out_rows = out_0.rearrange("(p t) c -> p t c", t=PACK)
        out_words = out_1[0].rearrange("p c r -> p (c r)").bitcast(I32)
        best = [sb("best%d" % j, [P, PACK, width], F32) for j, (c0, width) in enumerate(PARTS)]
        best_bf = [sb("best_bf%d" % j, [P, width, PACK], BF16) for j, (c0, width) in enumerate(PARTS)]

        def apply_gate(h, u):
            planes = slice(2 * u, 2 * u + 2)
            nc.vector.scalar_tensor_tensor(gated[h][:, planes, :], s_ps[h][u][:], 0.0625, gate[h][:, planes, :], ALU.mult, ALU.mult)

        def take_larger(j):
            c0, width = PARTS[j]
            h = c0 // HALF
            for planes in (slice(0, 2), slice(2, 4)) if j == 0 else (slice(0, 4),):
                nc.vector.tensor_tensor(
                    best[j][:, planes, :], gated[h][:, planes, c0 - h * HALF : c0 - h * HALF + width],
                    other[:, planes, c0 : c0 + width], ALU.max,
                )
            nc.sync.dma_start(out_rows[:, :, c0 : c0 + width], best[j][:])

        def weave(j, copy):
            copy(best_bf[j][:].rearrange("p (c i) t -> p c t i", i=4), best[j][:].rearrange("p t (c i) -> p c t i", i=4))

        def quantize_out(j):
            c0, width = PARTS[j]
            cols = slice(c0, c0 + width)
            nc.vector.quantize_mx(
                out=o_wd[:, cols].bitcast(FP8X4), scales=o_sc[:, cols], in_=best_bf[j][:].rearrange("p c t -> p (c t)")
            )

        def store_words(cols):
            nc.sync.dma_start(out_words[:, cols], o_wd[:, cols].bitcast(I32))

        take_larger(0)
        weave(0, nc.scalar.copy)
        apply_gate(1, 0)
        apply_gate(1, 1)
        take_larger(1)
        weave(1, nc.scalar.copy)
        take_larger(2)
        quantize_out(0)
        weave(2, nc.vector.tensor_copy)
        quantize_out(1)
        store_words(slice(0, PARTS[2][0]))
        quantize_out(2)
        store_words(slice(PARTS[2][0], S))
        for q in range(4):
            queue = nc.scalar if q % 2 else nc.sync
            queue.dma_start(out_2[0, 4 * q : 4 * q + 4, :].bitcast(I32), o_sc[32 * q : 32 * q + 4, :].bitcast(I32))
